import numpy as np
import ml_dtypes

BF16 = ml_dtypes.bfloat16


def bf(x):
    return np.asarray(x, np.float32).astype(BF16)


def f32(x):
    return np.asarray(x, np.float32)


def f64(x):
    return np.asarray(x).astype(np.float64)


def striped(idx):
    return np.concatenate([l.reshape(-1, 16).T for l in idx])


def rows(idx, k):
    return np.tile(np.repeat(idx, 16, axis=0), (k // (16 * 8), 1))


def look(tab, idx):
    return np.take_along_axis(f64(tab), rows(idx, len(tab)), axis=1)


K, S, V, N = 512, 2048, 1024, 1024


def setup_inputs():
    return {"tab": f32(np.random.standard_normal((K, S))), "y": f32(np.random.standard_normal((K, V))), "offs": striped(np.stack([np.random.permutation(S)[:N] for _ in range(8)]))}


def reference(tab, y, offs):
    idx = np.stack([g.T.reshape(-1) for g in np.split(offs, 8)])
    t = look(tab, idx)
    x = np.tanh(t) * f64(y)
    return x

@@ -1,0 +1,42 @@
+import concourse.mybir as mybir
+
+P = 128
+GROUP = 16
+PIECE = 512
+
+F32 = mybir.dt.float32
+U16 = mybir.dt.uint16
+TANH = mybir.ActivationFunctionType.Tanh
+MULT = mybir.AluOpType.mult
+
+
+def tile_lookup_gate_tanh_out_kernel(tc, tab, y, offs, out):
+    nc = tc.nc
+    rows, width = tab.shape
+    n = y.shape[1]
+    blocks = rows // P
+
+    with (
+        tc.tile_pool(name="lists", bufs=1) as lists,
+        tc.tile_pool(name="data", bufs=blocks) as data,
+    ):
+        offsets = lists.tile([P, n // GROUP], U16, name="offsets")
+        nc.sync.dma_start(offsets[:], offs)
+
+        windows, streams = [], []
+        for b in range(blocks):
+            window = data.tile([P, width], F32, name="window")
+            stream = data.tile([P, n], F32, name="stream")
+            nc.sync.dma_start(window[:], tab[b * P : (b + 1) * P, :])
+            nc.sync.dma_start(stream[:], y[b * P : (b + 1) * P, :])
+            windows.append(window)
+            streams.append(stream)
+
+        for b in range(blocks):
+            gate = data.tile([P, n], F32, name="gate")
+            result = data.tile([P, n], F32, name="result")
+            for j in range(0, n, PIECE):
+                picks = offsets[:, j // GROUP : (j + PIECE) // GROUP]
+                nc.scalar.activation(gate[:, j : j + PIECE], windows[b][:].indirect(picks), TANH)
+            nc.vector.tensor_tensor(result[:], gate[:], streams[b][:], MULT)
+            nc.sync.dma_start(out[b * P : (b + 1) * P, :], result[:])

@@ -21,16 +21,15 @@ def tile_lookup_gate_tanh_out_kernel(tc, tab, y, offs, out):
         tc.tile_pool(name="data", bufs=blocks) as data,
     ):
         offsets = lists.tile([P, n // GROUP], U16, name="offsets")
-        nc.sync.dma_start(offsets[:], offs)
+        windows = [data.tile([P, width], F32, name="window") for b in range(blocks)]
+        streams = [data.tile([P, n], F32, name="stream") for b in range(blocks)]
 
-        windows, streams = [], []
+        nc.sync.dma_start(windows[0][:], tab[0:P, :])
+        nc.sync.dma_start(offsets[:], offs)
         for b in range(blocks):
-            window = data.tile([P, width], F32, name="window")
-            stream = data.tile([P, n], F32, name="stream")
-            nc.sync.dma_start(window[:], tab[b * P : (b + 1) * P, :])
-            nc.sync.dma_start(stream[:], y[b * P : (b + 1) * P, :])
-            windows.append(window)
-            streams.append(stream)
+            if b + 1 < blocks:
+                nc.sync.dma_start(windows[b + 1][:], tab[(b + 1) * P : (b + 2) * P, :])
+            nc.sync.dma_start(streams[b][:], y[b * P : (b + 1) * P, :])
 
         for b in range(blocks):
             gate = data.tile([P, n], F32, name="gate")
@@ -38,5 +37,7 @@ def tile_lookup_gate_tanh_out_kernel(tc, tab, y, offs, out):
             for j in range(0, n, PIECE):
                 picks = offsets[:, j // GROUP : (j + PIECE) // GROUP]
                 nc.scalar.activation(gate[:, j : j + PIECE], windows[b][:].indirect(picks), TANH)
-            nc.vector.tensor_tensor(result[:], gate[:], streams[b][:], MULT)
+                nc.vector.tensor_tensor(
+                    result[:, j : j + PIECE], gate[:, j : j + PIECE], streams[b][:, j : j + PIECE], MULT
+                )
             nc.sync.dma_start(out[b * P : (b + 1) * P, :], result[:])

import concourse.mybir as mybir

P = 128
GROUP = 16
PIECE = 512

F32 = mybir.dt.float32
U16 = mybir.dt.uint16
TANH = mybir.ActivationFunctionType.Tanh
MULT = mybir.AluOpType.mult


def tile_lookup_gate_tanh_out_kernel(tc, tab, y, offs, out):
    nc = tc.nc
    rows, width = tab.shape
    n = y.shape[1]
    blocks = rows // P

    with (
        tc.tile_pool(name="lists", bufs=1) as lists,
        tc.tile_pool(name="data", bufs=blocks) as data,
    ):
        offsets = lists.tile([P, n // GROUP], U16, name="offsets")
        windows = [data.tile([P, width], F32, name="window") for b in range(blocks)]
        streams = [data.tile([P, n], F32, name="stream") for b in range(blocks)]

        nc.sync.dma_start(windows[0][:], tab[0:P, :])
        nc.sync.dma_start(offsets[:], offs)
        for b in range(blocks):
            if b + 1 < blocks:
                nc.sync.dma_start(windows[b + 1][:], tab[(b + 1) * P : (b + 2) * P, :])
            nc.sync.dma_start(streams[b][:], y[b * P : (b + 1) * P, :])

        for b in range(blocks):
            gate = data.tile([P, n], F32, name="gate")
            result = data.tile([P, n], F32, name="result")
            for j in range(0, n, PIECE):
                picks = offsets[:, j // GROUP : (j + PIECE) // GROUP]
                nc.scalar.activation(gate[:, j : j + PIECE], windows[b][:].indirect(picks), TANH)
                nc.vector.tensor_tensor(
                    result[:, j : j + PIECE], gate[:, j : j + PIECE], streams[b][:, j : j + PIECE], MULT
                )
            nc.sync.dma_start(out[b * P : (b + 1) * P, :], result[:])
